import numpy as np
import ml_dtypes


def mxq(x, axis, fmt="e4m3"):
    dtype, down = {"e4m3": (ml_dtypes.float8_e4m3fn, 7), "e5m2": (ml_dtypes.float8_e5m2, 14)}[fmt]
    v = np.moveaxis(np.asarray(x, np.float32).astype(ml_dtypes.bfloat16).astype(np.float64), axis, -1)
    blocks = v.reshape(v.shape[:-1] + (-1, 32))
    amax = np.abs(blocks).max(-1, keepdims=True)
    byte = np.maximum(np.where(amax > 0, np.frexp(amax)[1] - 1 + 127, 0) - down, 1)
    scale = np.exp2(byte - 127.0)
    codes = (blocks / scale).astype(np.float32).astype(dtype).astype(np.float64)
    return np.moveaxis((codes * scale).reshape(v.shape), -1, axis)


WIDE = False


def mx_kscale(k):
    if not WIDE:
        return np.ones(k)
    levels = np.array([10, -10, 5, -5, 0])
    if k % 512:
        return np.exp2(np.random.permutation(np.resize(levels, k // 32))).repeat(32)
    a = np.empty((k // 512, 16))
    for p in range(k // 512):
        a[p, :8] = np.random.permutation(np.resize(levels, 8))
        for g in range(8):
            far = levels[np.abs(levels - a[p, g]) >= 10]
            a[p, g + 8] = far[np.random.randint(len(far))]
    return np.exp2(a.ravel()).repeat(32)


def f64(x):
    return np.asarray(x).astype(np.float64)


def striped(idx):
    return np.tile(idx.reshape(-1, 16).T, (8, 1)).astype(np.uint16)


def unstriped(offs):
    return offs[:16].T.reshape(-1).astype(np.int64)


def d_silu(v):
    s = 1.0 / (1.0 + np.exp(-np.maximum(v, -700.0)))
    return s * (1.0 + v * (1.0 - s))


K, T, E, C, H, N = 256, 512, 2, 256, 1024, 1024


def by_expert(wq, xq):
    return np.concatenate([wq[e].T @ xq[:, e * C:(e + 1) * C] for e in range(E)], axis=1)


def setup_inputs():
    n = np.random.standard_normal
    s = mx_kscale(N)[:, None]
    u = mx_kscale(H)
    return {
        "dyT": (n((N, T)) * s).astype(np.float32),
        "a": n((H, E * C)).astype(np.float32),
        "w2": (n((E, N, H)) / np.sqrt(N) / s[None] * u[None, None, :]).astype(np.float32),
        "w1": (n((E, H, K)) / np.sqrt(H) / u[None, :, None]).astype(np.float32),
        "gate": np.tile(np.random.uniform(0.2, 1.0, E * C), (N, 1)).astype(np.float32),
        "offs": striped(np.random.permutation(T)[:E * C]),
    }


def reference(dyT, a, w2, w1, gate, offs):
    idx = unstriped(offs)
    gq = mxq(f64(gate) * f64(dyT)[:, idx], 0, "e4m3")
    dh = by_expert(mxq(f64(w2), 1, "e4m3"), gq)
    da = dh * d_silu(f64(a))
    dx = by_expert(mxq(f64(w1), 1, "e4m3"), mxq(da, 0, "e4m3"))
    out = np.zeros((K, T))
    out[:, idx] = dx
    return out

@@ -1,0 +1,293 @@
+from contextlib import ExitStack
+
+import concourse.mybir as mybir
+
+K, T, E, C, H, N = 256, 512, 2, 256, 1024, 1024
+FLOPS = 2 * E * C * (N * H + H * K)
+BYTES = 4 * (N * T + H * E * C + E * N * H + E * H * K + E * C + K * T) + 2 * 128 * (E * C // 16)
+
+F32 = mybir.dt.float32
+BF16 = mybir.dt.bfloat16
+U32 = mybir.dt.uint32
+U16 = mybir.dt.uint16
+U8 = mybir.dt.uint8
+FP8X4 = mybir.dt.float8_e4m3fn_x4
+MULT = mybir.AluOpType.mult
+SUBTRACT = mybir.AluOpType.subtract
+COPY = mybir.ActivationFunctionType.Copy
+SIGMOID = mybir.ActivationFunctionType.Sigmoid
+
+P = 128
+PACK = 4
+PASS = P * PACK
+HALF = 128
+COLS = 16
+
+
+def tile_moe_bdx_mlp_silu_kernel(tc, dyT, a, w2, w1, gate, offs, out):
+    nc = tc.nc
+    with ExitStack() as ctx:
+        keep = ctx.enter_context(tc.tile_pool(name="keep", bufs=1))
+        two = ctx.enter_context(tc.tile_pool(name="two", bufs=2))
+        three = ctx.enter_context(tc.tile_pool(name="three", bufs=3))
+        hid = ctx.enter_context(tc.psum_pool(name="hid", bufs=4))
+        res = ctx.enter_context(tc.psum_pool(name="res", bufs=1))
+
+        offsets = keep.tile([P, E * C // 16], U16, name="offsets")
+        gates = keep.tile([P, E * C], F32, name="gates")
+        dy = {}
+        for c in range(2):
+            for j in range(PACK):
+                dy[c, j] = keep.tile([P, T], F32, name=f"dy{c}{j}")
+        act = {}
+        for h in range(2):
+            act[h] = keep.tile([P, PACK, E * C], F32, name=f"act{h}")
+        w2_raw = {}
+        w1_raw = {}
+        for e in range(E):
+            for h in range(2):
+                w1_raw[e, h] = keep.tile([P, PACK, K], F32, name=f"w1raw{e}{h}")
+                for c in range(2):
+                    w2_raw[e, h, c] = keep.tile([P, PACK, PASS], F32, name=f"w2raw{e}{h}{c}")
+
+        def load_dy(c, j):
+            rows = dyT[c * PASS : (c + 1) * PASS, :].rearrange("(p j) t -> p j t", j=PACK)
+            nc.sync.dma_start(out=dy[c, j][:], in_=rows[:, j, :])
+
+        def load_w2(e, h, c, lo=0, hi=PASS):
+            rows = w2[e, c * PASS : (c + 1) * PASS, h * PASS + lo : h * PASS + hi]
+            nc.sync.dma_start(out=w2_raw[e, h, c][:, :, lo:hi], in_=rows.rearrange("(p j) i -> p j i", j=PACK))
+
+        def load_act(h):
+            rows = a[h * PASS : (h + 1) * PASS, :]
+            nc.sync.dma_start(out=act[h][:], in_=rows.rearrange("(p t) s -> p t s", t=PACK))
+
+        def load_w1(e, h):
+            rows = w1[e, h * PASS : (h + 1) * PASS, :]
+            nc.sync.dma_start(out=w1_raw[e, h][:], in_=rows.rearrange("(p j) k -> p j k", j=PACK))
+
+        nc.sync.dma_start(offsets[:], offs)
+        nc.sync.dma_start(out=gates[:], in_=gate[0:P, :])
+        load_dy(0, 0)
+        load_w2(0, 0, 0, 0, 256)
+        load_dy(0, 1)
+        load_dy(0, 2)
+        load_w2(0, 0, 0, 256, 512)
+        load_dy(0, 3)
+        for j in range(PACK):
+            load_dy(1, j)
+        load_act(0)
+        load_w2(0, 0, 1)
+        load_w2(0, 1, 0)
+        load_act(1)
+        load_w2(0, 1, 1)
+        load_w1(0, 0)
+        load_w1(0, 1)
+        load_w2(1, 0, 0)
+        load_w2(1, 0, 1)
+        load_w2(1, 1, 0)
+        load_w2(1, 1, 1)
+        load_w1(1, 0)
+        load_w1(1, 1)
+
+        seed = keep.tile([P, 1], F32, name="seed")
+        warm = keep.tile([P, 1], F32, name="warm")
+        nc.vector.memset(seed[:], 0.0)
+        nc.scalar.activation(warm[:], seed[:], SIGMOID)
+
+        g_f32, g_bf, g_codes, g_scales = {}, {}, {}, {}
+        w2_bf, w2_codes, w2_scales = {}, {}, {}
+        w1_bf, w1_codes, w1_scales = {}, {}, {}
+        sig, slope = {}, {}
+        da_bf, da_codes, da_scales = {}, {}, {}
+        for e in range(E):
+            for c in range(2):
+                g_codes[e, c] = keep.tile([P, C], U32, name=f"gcodes{e}{c}", align_bytes=64)
+                g_scales[e, c] = keep.tile([P, C], U8, name=f"gscales{e}{c}", align_bytes=64)
+                w1_codes[e, c] = keep.tile([P, K], U32, name=f"w1codes{e}{c}", align_bytes=64)
+                w1_scales[e, c] = keep.tile([P, K], U8, name=f"w1scales{e}{c}", align_bytes=64)
+                da_codes[e, c] = keep.tile([P, C], U32, name=f"dacodes{e}{c}", align_bytes=64)
+                da_scales[e, c] = keep.tile([P, C], U8, name=f"dascales{e}{c}", align_bytes=64)
+                for h in range(2):
+                    w2_codes[e, h, c] = keep.tile([P, PASS], U32, name=f"w2codes{e}{h}{c}", align_bytes=64)
+                    w2_scales[e, h, c] = keep.tile([P, PASS], U8, name=f"w2scales{e}{h}{c}", align_bytes=64)
+        sums = {}
+        placed = {}
+        for b in range(2):
+            placed[b] = keep.tile([P, T], F32, name=f"placed{b}")
+            for e in range(E):
+                sums[e, b] = res.tile([P, C], F32, name=f"sums{e}{b}")
+
+        def slots(e):
+            return slice(e * C, (e + 1) * C)
+
+        def list_of(e):
+            return offsets[:, e * COLS : (e + 1) * COLS]
+
+        def gather(e, c, j):
+            if j == 0:
+                g_f32[e, c] = three.tile([P, PACK, C], F32, name="g_f32")
+            nc.vector.tensor_tensor(g_f32[e, c][:, j, :], dy[c, j][:].indirect(list_of(e)), gates[:, slots(e)], MULT)
+
+        def round_g(e, c):
+            g_bf[e, c] = two.tile([P, C * PACK], BF16, name="g_bf", align_bytes=64)
+            nc.scalar.copy(
+                g_bf[e, c][:].rearrange("p (c i t) -> p c t i", i=4, t=PACK),
+                g_f32[e, c][:].rearrange("p t (c i) -> p c t i", i=4),
+            )
+
+        def quantize(codes, scales, values):
+            nc.vector.quantize_mx(out=codes.bitcast(FP8X4), scales=scales, in_=values)
+
+        def quant_g(e, c):
+            quantize(g_codes[e, c][:], g_scales[e, c][:], g_bf[e, c][:])
+
+        def round_w2(e, h, c, lo=0, hi=PASS):
+            if lo == 0:
+                w2_bf[e, h, c] = three.tile([P, PASS * PACK], BF16, name="w2_bf", align_bytes=64)
+            ms = slice(lo // PACK, hi // PACK)
+            nc.scalar.copy(
+                w2_bf[e, h, c][:].rearrange("p (t m j) -> p m j t", t=PACK, j=PACK)[:, ms],
+                w2_raw[e, h, c][:, :, lo:hi].rearrange("p j (m t) -> p m j t", t=PACK),
+            )
+
+        def quant_w2(e, h, c):
+            quantize(w2_codes[e, h, c][:], w2_scales[e, h, c][:], w2_bf[e, h, c][:])
+
+        def round_w1(e, h):
+            w1_bf[e, h] = two.tile([P, K * PACK], BF16, name="w1_bf", align_bytes=64)
+            nc.scalar.copy(
+                w1_bf[e, h][:].rearrange("p (c i j) -> p c j i", i=4, j=PACK),
+                w1_raw[e, h][:].rearrange("p j (c i) -> p c j i", i=4),
+            )
+
+        def quant_w1(e, h):
+            quantize(w1_codes[e, h][:], w1_scales[e, h][:], w1_bf[e, h][:])
+
+        def sigmoid(e, h):
+            sig[e, h] = two.tile([P, PACK, C], F32, name="sig")
+            nc.scalar.activation(sig[e, h][:], act[h][:, :, slots(e)], SIGMOID)
+
+        def slope_1(e, h):
+            slope[e, h] = keep.tile([P, PACK, C], F32, name=f"slope{e}{h}")
+            nc.vector.scalar_tensor_tensor(slope[e, h][:], sig[e, h][:], 1.0, act[h][:, :, slots(e)], SUBTRACT, MULT)
+
+        def slope_2(e, h):
+            nc.vector.scalar_tensor_tensor(slope[e, h][:], slope[e, h][:], 1.0, sig[e, h][:], SUBTRACT, MULT)
+
+        def first(e, h, s):
+            bank = hid.tile([P, PACK, HALF], F32, name="bank")
+            cols = slice(s * HALF, (s + 1) * HALF)
+            for t in range(PACK):
+                for c in range(2):
+                    rows = slice(t * P, (t + 1) * P)
+                    nc.tensor.matmul_mx(
+                        bank[:, t, :],
+                        lhsT=w2_codes[e, h, c][:, rows].bitcast(FP8X4),
+                        lhsT_scale=w2_scales[e, h, c][:, rows],
+                        rhs=g_codes[e, c][:, cols].bitcast(FP8X4),
+                        rhs_scale=g_scales[e, c][:, cols],
+                        start=(c == 0),
+                        stop=(c == 1),
+                    )
+            da_bf[e, h, s] = three.tile([P, HALF * PACK], BF16, name="da_bf", align_bytes=64)
+            nc.vector.tensor_tensor(
+                da_bf[e, h, s][:].rearrange("p (c i t) -> p c t i", i=4, t=PACK),
+                slope[e, h][:, :, cols].rearrange("p t (c i) -> p c t i", i=4),
+                bank[:].rearrange("p t (c i) -> p c t i", i=4),
+                MULT,
+            )
+
+        def quant_da(e, h, s):
+            cols = slice(s * HALF, (s + 1) * HALF)
+            quantize(da_codes[e, h][:, cols], da_scales[e, h][:, cols], da_bf[e, h, s][:])
+
+        def second(e, b):
+            rows = slice(b * P, (b + 1) * P)
+            for h in range(2):
+                nc.tensor.matmul_mx(
+                    sums[e, b][:],
+                    lhsT=w1_codes[e, h][:, rows].bitcast(FP8X4),
+                    lhsT_scale=w1_scales[e, h][:, rows],
+                    rhs=da_codes[e, h][:].bitcast(FP8X4),
+                    rhs_scale=da_scales[e, h][:],
+                    start=(h == 0),
+                    stop=(h == 1),
+                )
+            flat = two.tile([P, C], F32, name="flat")
+            nc.scalar.activation(flat[:], sums[e, b][:], COPY, scale=-1.0)
+            nc.vector.tensor_copy(placed[b][:].indirect(list_of(e)), flat[:])
+            if e == E - 1:
+                nc.sync.dma_start(out=out[rows, :], in_=placed[b][:])
+
+        for j in range(PACK):
+            for e in range(E):
+                gather(e, 0, j)
+        round_w2(0, 0, 0, 0, 256)
+        round_w2(0, 0, 0, 256, 512)
+        round_g(0, 0)
+        round_g(1, 0)
+        for j in range(PACK):
+            for e in range(E):
+                gather(e, 1, j)
+        quant_w2(0, 0, 0)
+        quant_g(0, 0)
+        quant_g(1, 0)
+        round_g(0, 1)
+        sigmoid(0, 0)
+        quant_g(0, 1)
+        round_w2(0, 0, 1)
+        slope_1(0, 0)
+        quant_w2(0, 0, 1)
+        slope_2(0, 0)
+        round_g(1, 1)
+        first(0, 0, 0)
+        first(0, 0, 1)
+        quant_g(1, 1)
+        sigmoid(1, 0)
+        quant_da(0, 0, 0)
+        quant_da(0, 0, 1)
+        round_w2(0, 1, 0)
+        slope_1(1, 0)
+        sigmoid(0, 1)
+        quant_w2(0, 1, 0)
+        round_w2(0, 1, 1)
+        slope_2(1, 0)
+        slope_1(0, 1)
+        quant_w2(0, 1, 1)
+        slope_2(0, 1)
+        round_w1(0, 0)
+        round_w1(0, 1)
+        first(0, 1, 0)
+        first(0, 1, 1)
+        quant_w1(0, 0)
+        quant_w1(0, 1)
+        quant_da(0, 1, 0)
+        quant_da(0, 1, 1)
+        second(0, 0)
+        second(0, 1)
+        round_w2(1, 0, 0)
+        quant_w2(1, 0, 0)
+        round_w2(1, 0, 1)
+        quant_w2(1, 0, 1)
+        sigmoid(1, 1)
+        slope_1(1, 1)
+        first(1, 0, 0)
+        first(1, 0, 1)
+        slope_2(1, 1)
+        quant_da(1, 0, 0)
+        quant_da(1, 0, 1)
+        round_w2(1, 1, 0)
+        quant_w2(1, 1, 0)
+        round_w2(1, 1, 1)
+        quant_w2(1, 1, 1)
+        first(1, 1, 0)
+        first(1, 1, 1)
+        round_w1(1, 0)
+        round_w1(1, 1)
+        quant_w1(1, 0)
+        quant_w1(1, 1)
+        quant_da(1, 1, 0)
+        quant_da(1, 1, 1)
+        second(1, 0)
+        second(1, 1)

@@ -3,8 +3,9 @@ from contextlib import ExitStack
 import concourse.mybir as mybir
 
 K, T, E, C, H, N = 256, 512, 2, 256, 1024, 1024
-FLOPS = 2 * E * C * (N * H + H * K)
-BYTES = 4 * (N * T + H * E * C + E * N * H + E * H * K + E * C + K * T) + 2 * 128 * (E * C // 16)
+SLOTS = E * C
+FLOPS = 2 * SLOTS * (N * H + H * K)
+BYTES = 4 * (N * T + H * SLOTS + E * N * H + E * H * K + SLOTS + K * T) + 2 * 128 * (SLOTS // 16)
 
 F32 = mybir.dt.float32
 BF16 = mybir.dt.bfloat16
@@ -15,13 +16,14 @@ FP8X4 = mybir.dt.float8_e4m3fn_x4
 MULT = mybir.AluOpType.mult
 SUBTRACT = mybir.AluOpType.subtract
 COPY = mybir.ActivationFunctionType.Copy
+SILU = mybir.ActivationFunctionType.Silu
 SIGMOID = mybir.ActivationFunctionType.Sigmoid
 
 P = 128
 PACK = 4
 PASS = P * PACK
-HALF = 128
-COLS = 16
+HALF = C // 2
+WINDOW = T + 32
 
 
 def tile_moe_bdx_mlp_silu_kernel(tc, dyT, a, w2, w1, gate, offs, out):
@@ -29,265 +31,249 @@ def tile_moe_bdx_mlp_silu_kernel(tc, dyT, a, w2, w1, gate, offs, out):
     with ExitStack() as ctx:
         keep = ctx.enter_context(tc.tile_pool(name="keep", bufs=1))
         two = ctx.enter_context(tc.tile_pool(name="two", bufs=2))
-        three = ctx.enter_context(tc.tile_pool(name="three", bufs=3))
-        hid = ctx.enter_context(tc.psum_pool(name="hid", bufs=4))
-        res = ctx.enter_context(tc.psum_pool(name="res", bufs=1))
+        four = ctx.enter_context(tc.tile_pool(name="four", bufs=4))
+        hidden = ctx.enter_context(tc.psum_pool(name="hidden", bufs=4))
+        result = ctx.enter_context(tc.psum_pool(name="result", bufs=1))
 
-        offsets = keep.tile([P, E * C // 16], U16, name="offsets")
-        gates = keep.tile([P, E * C], F32, name="gates")
-        dy = {}
+        offsets = keep.tile([P, SLOTS // 16], U16, name="offsets")
+        gates = keep.tile([P, SLOTS], F32, name="gates")
+        act = keep.tile([P, 2, PACK, SLOTS], F32, name="act")
+        slope = keep.tile([P, 2, PACK, SLOTS], F32, name="slope")
+        dy, w1_raw, w2_raw = {}, {}, {}
         for c in range(2):
             for j in range(PACK):
-                dy[c, j] = keep.tile([P, T], F32, name=f"dy{c}{j}")
-        act = {}
-        for h in range(2):
-            act[h] = keep.tile([P, PACK, E * C], F32, name=f"act{h}")
-        w2_raw = {}
-        w1_raw = {}
+                dy[c, j] = keep.tile([P, WINDOW], F32, name=f"dy{c}{j}")
         for e in range(E):
-            for h in range(2):
-                w1_raw[e, h] = keep.tile([P, PACK, K], F32, name=f"w1raw{e}{h}")
-                for c in range(2):
-                    w2_raw[e, h, c] = keep.tile([P, PACK, PASS], F32, name=f"w2raw{e}{h}{c}")
+            w1_raw[e] = keep.tile([P, 2, PACK, K], F32, name=f"w1_raw{e}")
+            for c in range(2):
+                w2_raw[e, c] = keep.tile([P, PACK, H], F32, name=f"w2_raw{e}{c}")
 
         def load_dy(c, j):
             rows = dyT[c * PASS : (c + 1) * PASS, :].rearrange("(p j) t -> p j t", j=PACK)
-            nc.sync.dma_start(out=dy[c, j][:], in_=rows[:, j, :])
+            nc.sync.dma_start(out=dy[c, j][:, :T], in_=rows[:, j, :])
 
-        def load_w2(e, h, c, lo=0, hi=PASS):
-            rows = w2[e, c * PASS : (c + 1) * PASS, h * PASS + lo : h * PASS + hi]
-            nc.sync.dma_start(out=w2_raw[e, h, c][:, :, lo:hi], in_=rows.rearrange("(p j) i -> p j i", j=PACK))
+        def load_act(h, u):
+            rows = a[h * PASS : (h + 1) * PASS, :].rearrange("(p t) s -> p t s", t=PACK)
+            ts = slice(2 * u, 2 * u + 2)
+            nc.sync.dma_start(out=act[:, h, ts, :], in_=rows[:, ts, :])
 
-        def load_act(h):
-            rows = a[h * PASS : (h + 1) * PASS, :]
-            nc.sync.dma_start(out=act[h][:], in_=rows.rearrange("(p t) s -> p t s", t=PACK))
+        def load_w2(e, c):
+            rows = w2[e, c * PASS : (c + 1) * PASS, :]
+            nc.sync.dma_start(out=w2_raw[e, c][:], in_=rows.rearrange("(p j) i -> p j i", j=PACK))
 
-        def load_w1(e, h):
-            rows = w1[e, h * PASS : (h + 1) * PASS, :]
-            nc.sync.dma_start(out=w1_raw[e, h][:], in_=rows.rearrange("(p j) k -> p j k", j=PACK))
+        def load_w1(e):
+            nc.sync.dma_start(out=w1_raw[e][:], in_=w1[e].rearrange("(h p j) k -> p h j k", h=2, j=PACK))
 
         nc.sync.dma_start(offsets[:], offs)
         nc.sync.dma_start(out=gates[:], in_=gate[0:P, :])
         load_dy(0, 0)
-        load_w2(0, 0, 0, 0, 256)
         load_dy(0, 1)
+        load_act(0, 0)
         load_dy(0, 2)
-        load_w2(0, 0, 0, 256, 512)
         load_dy(0, 3)
-        for j in range(PACK):
-            load_dy(1, j)
-        load_act(0)
-        load_w2(0, 0, 1)
-        load_w2(0, 1, 0)
-        load_act(1)
-        load_w2(0, 1, 1)
-        load_w1(0, 0)
-        load_w1(0, 1)
-        load_w2(1, 0, 0)
-        load_w2(1, 0, 1)
-        load_w2(1, 1, 0)
-        load_w2(1, 1, 1)
-        load_w1(1, 0)
-        load_w1(1, 1)
+        load_act(0, 1)
+        load_dy(1, 0)
+        load_dy(1, 1)
+        load_act(1, 0)
+        load_dy(1, 2)
+        load_act(1, 1)
+        load_dy(1, 3)
+        for e in range(E):
+            for c in range(2):
+                load_w2(e, c)
+        for e in range(E):
+            load_w1(e)
 
         seed = keep.tile([P, 1], F32, name="seed")
         warm = keep.tile([P, 1], F32, name="warm")
         nc.vector.memset(seed[:], 0.0)
         nc.scalar.activation(warm[:], seed[:], SIGMOID)
+        for c in range(2):
+            for j in range(PACK):
+                nc.gpsimd.memset(dy[c, j][:, T:], 0.0)
 
         g_f32, g_bf, g_codes, g_scales = {}, {}, {}, {}
         w2_bf, w2_codes, w2_scales = {}, {}, {}
         w1_bf, w1_codes, w1_scales = {}, {}, {}
-        sig, slope = {}, {}
         da_bf, da_codes, da_scales = {}, {}, {}
+        sums, flat, placed = {}, {}, {}
+        for c in range(2):
+            g_f32[c] = keep.tile([P, PACK, SLOTS], F32, name=f"g_f32{c}")
+            g_bf[c] = keep.tile([P, SLOTS * PACK], BF16, name=f"g_bf{c}", align_bytes=64)
+            g_codes[c] = keep.tile([P, SLOTS], U32, name=f"g_codes{c}", align_bytes=64)
+            g_scales[c] = keep.tile([P, SLOTS], U8, name=f"g_scales{c}", align_bytes=64)
+            placed[c] = keep.tile([P, T], F32, name=f"placed{c}")
         for e in range(E):
-            for c in range(2):
-                g_codes[e, c] = keep.tile([P, C], U32, name=f"gcodes{e}{c}", align_bytes=64)
-                g_scales[e, c] = keep.tile([P, C], U8, name=f"gscales{e}{c}", align_bytes=64)
-                w1_codes[e, c] = keep.tile([P, K], U32, name=f"w1codes{e}{c}", align_bytes=64)
-                w1_scales[e, c] = keep.tile([P, K], U8, name=f"w1scales{e}{c}", align_bytes=64)
-                da_codes[e, c] = keep.tile([P, C], U32, name=f"dacodes{e}{c}", align_bytes=64)
-                da_scales[e, c] = keep.tile([P, C], U8, name=f"dascales{e}{c}", align_bytes=64)
-                for h in range(2):
-                    w2_codes[e, h, c] = keep.tile([P, PASS], U32, name=f"w2codes{e}{h}{c}", align_bytes=64)
-                    w2_scales[e, h, c] = keep.tile([P, PASS], U8, name=f"w2scales{e}{h}{c}", align_bytes=64)
-        sums = {}
-        placed = {}
-        for b in range(2):
-            placed[b] = keep.tile([P, T], F32, name=f"placed{b}")
-            for e in range(E):
-                sums[e, b] = res.tile([P, C], F32, name=f"sums{e}{b}")
+            w1_bf[e] = keep.tile([P, 2 * K * PACK], BF16, name=f"w1_bf{e}", align_bytes=64)
+            w1_codes[e] = keep.tile([P, 2 * K], U32, name=f"w1_codes{e}", align_bytes=64)
+            w1_scales[e] = keep.tile([P, 2 * K], U8, name=f"w1_scales{e}", align_bytes=64)
+            for h in range(2):
+                da_codes[e, h] = keep.tile([P, C], U32, name=f"da_codes{e}{h}", align_bytes=64)
+                da_scales[e, h] = keep.tile([P, C], U8, name=f"da_scales{e}{h}", align_bytes=64)
+                for c in range(2):
+                    w2_codes[e, h, c] = keep.tile([P, PASS], U32, name=f"w2_codes{e}{h}{c}", align_bytes=64)
+                    w2_scales[e, h, c] = keep.tile([P, PASS], U8, name=f"w2_scales{e}{h}{c}", align_bytes=64)
+            for b in range(2):
+                sums[e, b] = result.tile([P, C], F32, name=f"sums{e}{b}")
+                flat[e, b] = keep.tile([P, C], F32, name=f"flat{e}{b}")
 
         def slots(e):
             return slice(e * C, (e + 1) * C)
 
-        def list_of(e):
-            return offsets[:, e * COLS : (e + 1) * COLS]
-
-        def gather(e, c, j):
-            if j == 0:
-                g_f32[e, c] = three.tile([P, PACK, C], F32, name="g_f32")
-            nc.vector.tensor_tensor(g_f32[e, c][:, j, :], dy[c, j][:].indirect(list_of(e)), gates[:, slots(e)], MULT)
-
-        def round_g(e, c):
-            g_bf[e, c] = two.tile([P, C * PACK], BF16, name="g_bf", align_bytes=64)
-            nc.scalar.copy(
-                g_bf[e, c][:].rearrange("p (c i t) -> p c t i", i=4, t=PACK),
-                g_f32[e, c][:].rearrange("p t (c i) -> p c t i", i=4),
-            )
-
         def quantize(codes, scales, values):
             nc.vector.quantize_mx(out=codes.bitcast(FP8X4), scales=scales, in_=values)
 
-        def quant_g(e, c):
-            quantize(g_codes[e, c][:], g_scales[e, c][:], g_bf[e, c][:])
+        def gather(c):
+            for j in range(PACK):
+                nc.vector.tensor_tensor(g_f32[c][:, j, :], dy[c, j][:].indirect(offsets[:]), gates[:], MULT)
 
-        def round_w2(e, h, c, lo=0, hi=PASS):
-            if lo == 0:
-                w2_bf[e, h, c] = three.tile([P, PASS * PACK], BF16, name="w2_bf", align_bytes=64)
-            ms = slice(lo // PACK, hi // PACK)
-            nc.scalar.copy(
-                w2_bf[e, h, c][:].rearrange("p (t m j) -> p m j t", t=PACK, j=PACK)[:, ms],
-                w2_raw[e, h, c][:, :, lo:hi].rearrange("p j (m t) -> p m j t", t=PACK),
+        def round_g(c, e, copy):
+            copy(
+                g_bf[c][:].rearrange("p (c i t) -> p c t i", i=4, t=PACK)[:, e * C // 4 : (e + 1) * C // 4],
+                g_f32[c][:, :, slots(e)].rearrange("p t (c i) -> p c t i", i=4),
             )
 
-        def quant_w2(e, h, c):
+        def quant_g(c):
+            quantize(g_codes[c][:], g_scales[c][:], g_bf[c][:])
+
+        def sigmoid(h, u):
+            ts = slice(2 * u, 2 * u + 2)
+            nc.scalar.activation(slope[:, h, ts, :], act[:, h, ts, :], SIGMOID)
+
+        def quarter(tile, e, x):
+            return tile[:].rearrange("p h (u x) s -> p (h u) x s", x=2)[:, :, x, slots(e)]
+
+        silus = {}
+
+        def silu(e, x):
+            silus[e, x] = two.tile([P, 4, C], F32, name="silu_t")
+            nc.scalar.activation(silus[e, x][:], quarter(act, e, x), SILU, scale=-1.0)
+
+        def derivative(e, x):
+            nc.vector.scalar_tensor_tensor(quarter(slope, e, x), silus[e, x][:], 1.0, quarter(slope, e, x), SUBTRACT, MULT)
+
+        def round_w2_planes(e, h, c, t0, t1, copy):
+            copy(
+                w2_bf[e, h, c][:].rearrange("p (t m j) -> p m j t", t=PACK, j=PACK)[:, :, :, t0:t1],
+                w2_raw[e, c][:, :, h * PASS : (h + 1) * PASS].rearrange("p j (m t) -> p m j t", t=PACK)[:, :, :, t0:t1],
+            )
+
+        def round_w2(e, h, c, shared):
+            w2_bf[e, h, c] = four.tile([P, PASS * PACK], BF16, name="w2_bf", align_bytes=64)
+            if shared:
+                round_w2_planes(e, h, c, 0, 2, nc.scalar.copy)
+                round_w2_planes(e, h, c, 2, 4, nc.vector.tensor_copy)
+            else:
+                round_w2_planes(e, h, c, 0, 4, nc.scalar.copy)
             quantize(w2_codes[e, h, c][:], w2_scales[e, h, c][:], w2_bf[e, h, c][:])
 
-        def round_w1(e, h):
-            w1_bf[e, h] = two.tile([P, K * PACK], BF16, name="w1_bf", align_bytes=64)
-            nc.scalar.copy(
-                w1_bf[e, h][:].rearrange("p (c i j) -> p c j i", i=4, j=PACK),
-                w1_raw[e, h][:].rearrange("p j (c i) -> p c j i", i=4),
-            )
-
-        def quant_w1(e, h):
-            quantize(w1_codes[e, h][:], w1_scales[e, h][:], w1_bf[e, h][:])
-
-        def sigmoid(e, h):
-            sig[e, h] = two.tile([P, PACK, C], F32, name="sig")
-            nc.scalar.activation(sig[e, h][:], act[h][:, :, slots(e)], SIGMOID)
-
-        def slope_1(e, h):
-            slope[e, h] = keep.tile([P, PACK, C], F32, name=f"slope{e}{h}")
-            nc.vector.scalar_tensor_tensor(slope[e, h][:], sig[e, h][:], 1.0, act[h][:, :, slots(e)], SUBTRACT, MULT)
-
-        def slope_2(e, h):
-            nc.vector.scalar_tensor_tensor(slope[e, h][:], slope[e, h][:], 1.0, sig[e, h][:], SUBTRACT, MULT)
-
-        def first(e, h, s):
-            bank = hid.tile([P, PACK, HALF], F32, name="bank")
-            cols = slice(s * HALF, (s + 1) * HALF)
-            for t in range(PACK):
-                for c in range(2):
+        def first(e, h):
+            banks = []
+            for s in range(2):
+                bank = hidden.tile([P, PACK, HALF], F32, name="bank")
+                banks.append(bank)
+                cols = slice(e * C + s * HALF, e * C + (s + 1) * HALF)
+                for t in range(PACK):
                     rows = slice(t * P, (t + 1) * P)
-                    nc.tensor.matmul_mx(
-                        bank[:, t, :],
-                        lhsT=w2_codes[e, h, c][:, rows].bitcast(FP8X4),
-                        lhsT_scale=w2_scales[e, h, c][:, rows],
-                        rhs=g_codes[e, c][:, cols].bitcast(FP8X4),
-                        rhs_scale=g_scales[e, c][:, cols],
-                        start=(c == 0),
-                        stop=(c == 1),
-                    )
-            da_bf[e, h, s] = three.tile([P, HALF * PACK], BF16, name="da_bf", align_bytes=64)
-            nc.vector.tensor_tensor(
-                da_bf[e, h, s][:].rearrange("p (c i t) -> p c t i", i=4, t=PACK),
-                slope[e, h][:, :, cols].rearrange("p t (c i) -> p c t i", i=4),
-                bank[:].rearrange("p t (c i) -> p c t i", i=4),
-                MULT,
+                    for c in range(2):
+                        nc.tensor.matmul_mx(
+                            bank[:, t, :],
+                            lhsT=w2_codes[e, h, c][:, rows].bitcast(FP8X4),
+                            lhsT_scale=w2_scales[e, h, c][:, rows],
+                            rhs=g_codes[c][:, cols].bitcast(FP8X4),
+                            rhs_scale=g_scales[c][:, cols],
+                            start=(c == 0),
+                            stop=(c == 1),
+                        )
+            da = two.tile([P, C * PACK], BF16, name="da", align_bytes=64)
+            for s in range(2):
+                cols = slice(e * C + s * HALF, e * C + (s + 1) * HALF)
+                nc.vector.tensor_tensor(
+                    da[:].rearrange("p (c i t) -> p c t i", i=4, t=PACK)[:, s * HALF // 4 : (s + 1) * HALF // 4],
+                    slope[:, h, :, cols].rearrange("p t (c i) -> p c t i", i=4),
+                    banks[s][:].rearrange("p t (c i) -> p c t i", i=4),
+                    MULT,
+                )
+            pieces = 2 if e == 1 else 1
+            w = C // pieces
+            for i in range(pieces):
+                cols = slice(i * w, (i + 1) * w)
+                quantize(da_codes[e, h][:, cols], da_scales[e, h][:, cols], da[:, i * w * PACK : (i + 1) * w * PACK])
+
+        def round_w1(e, h, copy):
+            copy(
+                w1_bf[e][:, h * K * PACK : (h + 1) * K * PACK].rearrange("p (c i j) -> p c j i", i=4, j=PACK),
+                w1_raw[e][:, h].rearrange("p j (c i) -> p c j i", i=4),
             )
 
-        def quant_da(e, h, s):
-            cols = slice(s * HALF, (s + 1) * HALF)
-            quantize(da_codes[e, h][:, cols], da_scales[e, h][:, cols], da_bf[e, h, s][:])
+        def quant_w1(e):
+            quantize(w1_codes[e][:], w1_scales[e][:], w1_bf[e][:])
 
-        def second(e, b):
-            rows = slice(b * P, (b + 1) * P)
-            for h in range(2):
-                nc.tensor.matmul_mx(
-                    sums[e, b][:],
-                    lhsT=w1_codes[e, h][:, rows].bitcast(FP8X4),
-                    lhsT_scale=w1_scales[e, h][:, rows],
-                    rhs=da_codes[e, h][:].bitcast(FP8X4),
-                    rhs_scale=da_scales[e, h][:],
-                    start=(h == 0),
-                    stop=(h == 1),
-                )
-            flat = two.tile([P, C], F32, name="flat")
-            nc.scalar.activation(flat[:], sums[e, b][:], COPY, scale=-1.0)
-            nc.vector.tensor_copy(placed[b][:].indirect(list_of(e)), flat[:])
-            if e == E - 1:
-                nc.sync.dma_start(out=out[rows, :], in_=placed[b][:])
+        def second(e):
+            pieces = 2 if e == 1 else 1
+            w = C // pieces
+            for i in range(pieces):
+                cols = slice(i * w, (i + 1) * w)
+                for b in range(2):
+                    for h in range(2):
+                        rows = slice(h * K + b * P, h * K + (b + 1) * P)
+                        nc.tensor.matmul_mx(
+                            sums[e, b][:, cols],
+                            lhsT=w1_codes[e][:, rows].bitcast(FP8X4),
+                            lhsT_scale=w1_scales[e][:, rows],
+                            rhs=da_codes[e, h][:, cols].bitcast(FP8X4),
+                            rhs_scale=da_scales[e, h][:, cols],
+                            start=(h == 0),
+                            stop=(h == 1),
+                        )
+                    nc.scalar.activation(flat[e, b][:, cols], sums[e, b][:, cols], COPY, scale=-1.0)
+            for b in range(2):
+                for i in range(pieces):
+                    cols = slice(i * w, (i + 1) * w)
+                    entries = slice((e * C + i * w) // 16, (e * C + (i + 1) * w) // 16)
+                    nc.vector.tensor_copy(placed[b][:].indirect(offsets[:, entries]), flat[e, b][:, cols])
 
-        for j in range(PACK):
-            for e in range(E):
-                gather(e, 0, j)
-        round_w2(0, 0, 0, 0, 256)
-        round_w2(0, 0, 0, 256, 512)
-        round_g(0, 0)
-        round_g(1, 0)
-        for j in range(PACK):
-            for e in range(E):
-                gather(e, 1, j)
-        quant_w2(0, 0, 0)
-        quant_g(0, 0)
-        quant_g(1, 0)
-        round_g(0, 1)
+        S = nc.scalar.copy
+        V = nc.vector.tensor_copy
+        gather(0)
         sigmoid(0, 0)
-        quant_g(0, 1)
-        round_w2(0, 0, 1)
-        slope_1(0, 0)
-        quant_w2(0, 0, 1)
-        slope_2(0, 0)
-        round_g(1, 1)
-        first(0, 0, 0)
-        first(0, 0, 1)
-        quant_g(1, 1)
-        sigmoid(1, 0)
-        quant_da(0, 0, 0)
-        quant_da(0, 0, 1)
-        round_w2(0, 1, 0)
-        slope_1(1, 0)
         sigmoid(0, 1)
-        quant_w2(0, 1, 0)
-        round_w2(0, 1, 1)
-        slope_2(1, 0)
-        slope_1(0, 1)
-        quant_w2(0, 1, 1)
-        slope_2(0, 1)
-        round_w1(0, 0)
-        round_w1(0, 1)
-        first(0, 1, 0)
-        first(0, 1, 1)
-        quant_w1(0, 0)
-        quant_w1(0, 1)
-        quant_da(0, 1, 0)
-        quant_da(0, 1, 1)
-        second(0, 0)
-        second(0, 1)
-        round_w2(1, 0, 0)
-        quant_w2(1, 0, 0)
-        round_w2(1, 0, 1)
-        quant_w2(1, 0, 1)
+        round_g(0, 0, S)
+        round_g(0, 1, V)
+        quant_g(0)
+        gather(1)
+        sigmoid(1, 0)
         sigmoid(1, 1)
-        slope_1(1, 1)
-        first(1, 0, 0)
-        first(1, 0, 1)
-        slope_2(1, 1)
-        quant_da(1, 0, 0)
-        quant_da(1, 0, 1)
-        round_w2(1, 1, 0)
-        quant_w2(1, 1, 0)
-        round_w2(1, 1, 1)
-        quant_w2(1, 1, 1)
-        first(1, 1, 0)
-        first(1, 1, 1)
-        round_w1(1, 0)
-        round_w1(1, 1)
-        quant_w1(1, 0)
-        quant_w1(1, 1)
-        quant_da(1, 1, 0)
-        quant_da(1, 1, 1)
-        second(1, 0)
-        second(1, 1)
+        silu(0, 0)
+        round_g(1, 0, V)
+        round_g(1, 1, V)
+        quant_g(1)
+        derivative(0, 0)
+        silu(0, 1)
+        derivative(0, 1)
+        round_w2(0, 1, 0, False)
+        round_w2(0, 0, 0, True)
+        silu(1, 0)
+        derivative(1, 0)
+        round_w2(0, 0, 1, True)
+        round_w2(0, 1, 1, True)
+        first(0, 0)
+        first(0, 1)
+        silu(1, 1)
+        derivative(1, 1)
+        round_w2(1, 0, 0, True)
+        round_w2(1, 1, 0, False)
+        round_w2(1, 0, 1, True)
+        round_w2(1, 1, 1, False)
+        round_w1(0, 0, V)
+        round_w1(0, 1, S)
+        quant_w1(0)
+        first(1, 0)
+        first(1, 1)
+        round_w1(1, 0, S)
+        round_w1(1, 1, S)
+        quant_w1(1)
+        second(0)
+        second(1)
+        for b in range(2):
+            nc.sync.dma_start(out=out[b * P : (b + 1) * P, :], in_=placed[b][:])

@@ -30,8 +30,8 @@ def tile_moe_bdx_mlp_silu_kernel(tc, dyT, a, w2, w1, gate, offs, out):
     nc = tc.nc
     with ExitStack() as ctx:
         keep = ctx.enter_context(tc.tile_pool(name="keep", bufs=1))
-        two = ctx.enter_context(tc.tile_pool(name="two", bufs=2))
-        four = ctx.enter_context(tc.tile_pool(name="four", bufs=4))
+        two = ctx.enter_context(tc.tile_pool(name="two", bufs=4))
+        four = ctx.enter_context(tc.tile_pool(name="four", bufs=6))
         hidden = ctx.enter_context(tc.psum_pool(name="hidden", bufs=4))
         result = ctx.enter_context(tc.psum_pool(name="result", bufs=1))
 
@@ -61,28 +61,30 @@ def tile_moe_bdx_mlp_silu_kernel(tc, dyT, a, w2, w1, gate, offs, out):
             rows = w2[e, c * PASS : (c + 1) * PASS, :]
             nc.sync.dma_start(out=w2_raw[e, c][:], in_=rows.rearrange("(p j) i -> p j i", j=PACK))
 
-        def load_w1(e):
-            nc.sync.dma_start(out=w1_raw[e][:], in_=w1[e].rearrange("(h p j) k -> p h j k", h=2, j=PACK))
+        def load_w1(e, h):
+            rows = w1[e, h * PASS : (h + 1) * PASS, :]
+            nc.sync.dma_start(out=w1_raw[e][:, h], in_=rows.rearrange("(p j) k -> p j k", j=PACK))
 
         nc.sync.dma_start(offsets[:], offs)
         nc.sync.dma_start(out=gates[:], in_=gate[0:P, :])
         load_dy(0, 0)
         load_dy(0, 1)
-        load_act(0, 0)
         load_dy(0, 2)
+        load_act(0, 0)
         load_dy(0, 3)
         load_act(0, 1)
         load_dy(1, 0)
-        load_dy(1, 1)
         load_act(1, 0)
-        load_dy(1, 2)
+        load_dy(1, 1)
         load_act(1, 1)
+        load_dy(1, 2)
         load_dy(1, 3)
         for e in range(E):
             for c in range(2):
                 load_w2(e, c)
         for e in range(E):
-            load_w1(e)
+            for h in range(2):
+                load_w1(e, h)
 
         seed = keep.tile([P, 1], F32, name="seed")
         warm = keep.tile([P, 1], F32, name="warm")
@@ -140,17 +142,14 @@ def tile_moe_bdx_mlp_silu_kernel(tc, dyT, a, w2, w1, gate, offs, out):
             ts = slice(2 * u, 2 * u + 2)
             nc.scalar.activation(slope[:, h, ts, :], act[:, h, ts, :], SIGMOID)
 
-        def quarter(tile, e, x):
-            return tile[:].rearrange("p h (u x) s -> p (h u) x s", x=2)[:, :, x, slots(e)]
+        def part(tile, e):
+            return tile[:].rearrange("p h t s -> p (h t) s")[:, :, slots(e)]
 
-        silus = {}
+        def silu(e):
+            nc.scalar.activation(part(act, e), part(act, e), SILU, scale=-1.0)
 
-        def silu(e, x):
-            silus[e, x] = two.tile([P, 4, C], F32, name="silu_t")
-            nc.scalar.activation(silus[e, x][:], quarter(act, e, x), SILU, scale=-1.0)
-
-        def derivative(e, x):
-            nc.vector.scalar_tensor_tensor(quarter(slope, e, x), silus[e, x][:], 1.0, quarter(slope, e, x), SUBTRACT, MULT)
+        def derivative(e):
+            nc.vector.scalar_tensor_tensor(part(slope, e), part(act, e), 1.0, part(slope, e), SUBTRACT, MULT)
 
         def round_w2_planes(e, h, c, t0, t1, copy):
             copy(
@@ -238,33 +237,29 @@ def tile_moe_bdx_mlp_silu_kernel(tc, dyT, a, w2, w1, gate, offs, out):
         gather(0)
         sigmoid(0, 0)
         sigmoid(0, 1)
+        sigmoid(1, 0)
+        sigmoid(1, 1)
         round_g(0, 0, S)
         round_g(0, 1, V)
         quant_g(0)
+        silu(0)
         gather(1)
-        sigmoid(1, 0)
-        sigmoid(1, 1)
-        silu(0, 0)
+        derivative(0)
         round_g(1, 0, V)
         round_g(1, 1, V)
         quant_g(1)
-        derivative(0, 0)
-        silu(0, 1)
-        derivative(0, 1)
-        round_w2(0, 1, 0, False)
+        silu(1)
         round_w2(0, 0, 0, True)
-        silu(1, 0)
-        derivative(1, 0)
+        round_w2(0, 1, 0, False)
+        derivative(1)
         round_w2(0, 0, 1, True)
         round_w2(0, 1, 1, True)
         first(0, 0)
         first(0, 1)
-        silu(1, 1)
-        derivative(1, 1)
         round_w2(1, 0, 0, True)
         round_w2(1, 1, 0, False)
         round_w2(1, 0, 1, True)
-        round_w2(1, 1, 1, False)
+        round_w2(1, 1, 1, True)
         round_w1(0, 0, V)
         round_w1(0, 1, S)
         quant_w1(0)

from contextlib import ExitStack

import concourse.mybir as mybir

K, T, E, C, H, N = 256, 512, 2, 256, 1024, 1024
SLOTS = E * C
FLOPS = 2 * SLOTS * (N * H + H * K)
BYTES = 4 * (N * T + H * SLOTS + E * N * H + E * H * K + SLOTS + K * T) + 2 * 128 * (SLOTS // 16)

F32 = mybir.dt.float32
BF16 = mybir.dt.bfloat16
U32 = mybir.dt.uint32
U16 = mybir.dt.uint16
U8 = mybir.dt.uint8
FP8X4 = mybir.dt.float8_e4m3fn_x4
MULT = mybir.AluOpType.mult
SUBTRACT = mybir.AluOpType.subtract
COPY = mybir.ActivationFunctionType.Copy
SILU = mybir.ActivationFunctionType.Silu
SIGMOID = mybir.ActivationFunctionType.Sigmoid

P = 128
PACK = 4
PASS = P * PACK
HALF = C // 2
WINDOW = T + 32


def tile_moe_bdx_mlp_silu_kernel(tc, dyT, a, w2, w1, gate, offs, out):
    nc = tc.nc
    with ExitStack() as ctx:
        keep = ctx.enter_context(tc.tile_pool(name="keep", bufs=1))
        two = ctx.enter_context(tc.tile_pool(name="two", bufs=4))
        four = ctx.enter_context(tc.tile_pool(name="four", bufs=6))
        hidden = ctx.enter_context(tc.psum_pool(name="hidden", bufs=4))
        result = ctx.enter_context(tc.psum_pool(name="result", bufs=1))

        offsets = keep.tile([P, SLOTS // 16], U16, name="offsets")
        gates = keep.tile([P, SLOTS], F32, name="gates")
        act = keep.tile([P, 2, PACK, SLOTS], F32, name="act")
        slope = keep.tile([P, 2, PACK, SLOTS], F32, name="slope")
        dy, w1_raw, w2_raw = {}, {}, {}
        for c in range(2):
            for j in range(PACK):
                dy[c, j] = keep.tile([P, WINDOW], F32, name=f"dy{c}{j}")
        for e in range(E):
            w1_raw[e] = keep.tile([P, 2, PACK, K], F32, name=f"w1_raw{e}")
            for c in range(2):
                w2_raw[e, c] = keep.tile([P, PACK, H], F32, name=f"w2_raw{e}{c}")

        def load_dy(c, j):
            rows = dyT[c * PASS : (c + 1) * PASS, :].rearrange("(p j) t -> p j t", j=PACK)
            nc.sync.dma_start(out=dy[c, j][:, :T], in_=rows[:, j, :])

        def load_act(h, u):
            rows = a[h * PASS : (h + 1) * PASS, :].rearrange("(p t) s -> p t s", t=PACK)
            ts = slice(2 * u, 2 * u + 2)
            nc.sync.dma_start(out=act[:, h, ts, :], in_=rows[:, ts, :])

        def load_w2(e, c):
            rows = w2[e, c * PASS : (c + 1) * PASS, :]
            nc.sync.dma_start(out=w2_raw[e, c][:], in_=rows.rearrange("(p j) i -> p j i", j=PACK))

        def load_w1(e, h):
            rows = w1[e, h * PASS : (h + 1) * PASS, :]
            nc.sync.dma_start(out=w1_raw[e][:, h], in_=rows.rearrange("(p j) k -> p j k", j=PACK))

        nc.sync.dma_start(offsets[:], offs)
        nc.sync.dma_start(out=gates[:], in_=gate[0:P, :])
        load_dy(0, 0)
        load_dy(0, 1)
        load_dy(0, 2)
        load_act(0, 0)
        load_dy(0, 3)
        load_act(0, 1)
        load_dy(1, 0)
        load_act(1, 0)
        load_dy(1, 1)
        load_act(1, 1)
        load_dy(1, 2)
        load_dy(1, 3)
        for e in range(E):
            for c in range(2):
                load_w2(e, c)
        for e in range(E):
            for h in range(2):
                load_w1(e, h)

        seed = keep.tile([P, 1], F32, name="seed")
        warm = keep.tile([P, 1], F32, name="warm")
        nc.vector.memset(seed[:], 0.0)
        nc.scalar.activation(warm[:], seed[:], SIGMOID)
        for c in range(2):
            for j in range(PACK):
                nc.gpsimd.memset(dy[c, j][:, T:], 0.0)

        g_f32, g_bf, g_codes, g_scales = {}, {}, {}, {}
        w2_bf, w2_codes, w2_scales = {}, {}, {}
        w1_bf, w1_codes, w1_scales = {}, {}, {}
        da_bf, da_codes, da_scales = {}, {}, {}
        sums, flat, placed = {}, {}, {}
        for c in range(2):
            g_f32[c] = keep.tile([P, PACK, SLOTS], F32, name=f"g_f32{c}")
            g_bf[c] = keep.tile([P, SLOTS * PACK], BF16, name=f"g_bf{c}", align_bytes=64)
            g_codes[c] = keep.tile([P, SLOTS], U32, name=f"g_codes{c}", align_bytes=64)
            g_scales[c] = keep.tile([P, SLOTS], U8, name=f"g_scales{c}", align_bytes=64)
            placed[c] = keep.tile([P, T], F32, name=f"placed{c}")
        for e in range(E):
            w1_bf[e] = keep.tile([P, 2 * K * PACK], BF16, name=f"w1_bf{e}", align_bytes=64)
            w1_codes[e] = keep.tile([P, 2 * K], U32, name=f"w1_codes{e}", align_bytes=64)
            w1_scales[e] = keep.tile([P, 2 * K], U8, name=f"w1_scales{e}", align_bytes=64)
            for h in range(2):
                da_codes[e, h] = keep.tile([P, C], U32, name=f"da_codes{e}{h}", align_bytes=64)
                da_scales[e, h] = keep.tile([P, C], U8, name=f"da_scales{e}{h}", align_bytes=64)
                for c in range(2):
                    w2_codes[e, h, c] = keep.tile([P, PASS], U32, name=f"w2_codes{e}{h}{c}", align_bytes=64)
                    w2_scales[e, h, c] = keep.tile([P, PASS], U8, name=f"w2_scales{e}{h}{c}", align_bytes=64)
            for b in range(2):
                sums[e, b] = result.tile([P, C], F32, name=f"sums{e}{b}")
                flat[e, b] = keep.tile([P, C], F32, name=f"flat{e}{b}")

        def slots(e):
            return slice(e * C, (e + 1) * C)

        def quantize(codes, scales, values):
            nc.vector.quantize_mx(out=codes.bitcast(FP8X4), scales=scales, in_=values)

        def gather(c):
            for j in range(PACK):
                nc.vector.tensor_tensor(g_f32[c][:, j, :], dy[c, j][:].indirect(offsets[:]), gates[:], MULT)

        def round_g(c, e, copy):
            copy(
                g_bf[c][:].rearrange("p (c i t) -> p c t i", i=4, t=PACK)[:, e * C // 4 : (e + 1) * C // 4],
                g_f32[c][:, :, slots(e)].rearrange("p t (c i) -> p c t i", i=4),
            )

        def quant_g(c):
            quantize(g_codes[c][:], g_scales[c][:], g_bf[c][:])

        def sigmoid(h, u):
            ts = slice(2 * u, 2 * u + 2)
            nc.scalar.activation(slope[:, h, ts, :], act[:, h, ts, :], SIGMOID)

        def part(tile, e):
            return tile[:].rearrange("p h t s -> p (h t) s")[:, :, slots(e)]

        def silu(e):
            nc.scalar.activation(part(act, e), part(act, e), SILU, scale=-1.0)

        def derivative(e):
            nc.vector.scalar_tensor_tensor(part(slope, e), part(act, e), 1.0, part(slope, e), SUBTRACT, MULT)

        def round_w2_planes(e, h, c, t0, t1, copy):
            copy(
                w2_bf[e, h, c][:].rearrange("p (t m j) -> p m j t", t=PACK, j=PACK)[:, :, :, t0:t1],
                w2_raw[e, c][:, :, h * PASS : (h + 1) * PASS].rearrange("p j (m t) -> p m j t", t=PACK)[:, :, :, t0:t1],
            )

        def round_w2(e, h, c, shared):
            w2_bf[e, h, c] = four.tile([P, PASS * PACK], BF16, name="w2_bf", align_bytes=64)
            if shared:
                round_w2_planes(e, h, c, 0, 2, nc.scalar.copy)
                round_w2_planes(e, h, c, 2, 4, nc.vector.tensor_copy)
            else:
                round_w2_planes(e, h, c, 0, 4, nc.scalar.copy)
            quantize(w2_codes[e, h, c][:], w2_scales[e, h, c][:], w2_bf[e, h, c][:])

        def first(e, h):
            banks = []
            for s in range(2):
                bank = hidden.tile([P, PACK, HALF], F32, name="bank")
                banks.append(bank)
                cols = slice(e * C + s * HALF, e * C + (s + 1) * HALF)
                for t in range(PACK):
                    rows = slice(t * P, (t + 1) * P)
                    for c in range(2):
                        nc.tensor.matmul_mx(
                            bank[:, t, :],
                            lhsT=w2_codes[e, h, c][:, rows].bitcast(FP8X4),
                            lhsT_scale=w2_scales[e, h, c][:, rows],
                            rhs=g_codes[c][:, cols].bitcast(FP8X4),
                            rhs_scale=g_scales[c][:, cols],
                            start=(c == 0),
                            stop=(c == 1),
                        )
            da = two.tile([P, C * PACK], BF16, name="da", align_bytes=64)
            for s in range(2):
                cols = slice(e * C + s * HALF, e * C + (s + 1) * HALF)
                nc.vector.tensor_tensor(
                    da[:].rearrange("p (c i t) -> p c t i", i=4, t=PACK)[:, s * HALF // 4 : (s + 1) * HALF // 4],
                    slope[:, h, :, cols].rearrange("p t (c i) -> p c t i", i=4),
                    banks[s][:].rearrange("p t (c i) -> p c t i", i=4),
                    MULT,
                )
            pieces = 2 if e == 1 else 1
            w = C // pieces
            for i in range(pieces):
                cols = slice(i * w, (i + 1) * w)
                quantize(da_codes[e, h][:, cols], da_scales[e, h][:, cols], da[:, i * w * PACK : (i + 1) * w * PACK])

        def round_w1(e, h, copy):
            copy(
                w1_bf[e][:, h * K * PACK : (h + 1) * K * PACK].rearrange("p (c i j) -> p c j i", i=4, j=PACK),
                w1_raw[e][:, h].rearrange("p j (c i) -> p c j i", i=4),
            )

        def quant_w1(e):
            quantize(w1_codes[e][:], w1_scales[e][:], w1_bf[e][:])

        def second(e):
            pieces = 2 if e == 1 else 1
            w = C // pieces
            for i in range(pieces):
                cols = slice(i * w, (i + 1) * w)
                for b in range(2):
                    for h in range(2):
                        rows = slice(h * K + b * P, h * K + (b + 1) * P)
                        nc.tensor.matmul_mx(
                            sums[e, b][:, cols],
                            lhsT=w1_codes[e][:, rows].bitcast(FP8X4),
                            lhsT_scale=w1_scales[e][:, rows],
                            rhs=da_codes[e, h][:, cols].bitcast(FP8X4),
                            rhs_scale=da_scales[e, h][:, cols],
                            start=(h == 0),
                            stop=(h == 1),
                        )
                    nc.scalar.activation(flat[e, b][:, cols], sums[e, b][:, cols], COPY, scale=-1.0)
            for b in range(2):
                for i in range(pieces):
                    cols = slice(i * w, (i + 1) * w)
                    entries = slice((e * C + i * w) // 16, (e * C + (i + 1) * w) // 16)
                    nc.vector.tensor_copy(placed[b][:].indirect(offsets[:, entries]), flat[e, b][:, cols])

        S = nc.scalar.copy
        V = nc.vector.tensor_copy
        gather(0)
        sigmoid(0, 0)
        sigmoid(0, 1)
        sigmoid(1, 0)
        sigmoid(1, 1)
        round_g(0, 0, S)
        round_g(0, 1, V)
        quant_g(0)
        silu(0)
        gather(1)
        derivative(0)
        round_g(1, 0, V)
        round_g(1, 1, V)
        quant_g(1)
        silu(1)
        round_w2(0, 0, 0, True)
        round_w2(0, 1, 0, False)
        derivative(1)
        round_w2(0, 0, 1, True)
        round_w2(0, 1, 1, True)
        first(0, 0)
        first(0, 1)
        round_w2(1, 0, 0, True)
        round_w2(1, 1, 0, False)
        round_w2(1, 0, 1, True)
        round_w2(1, 1, 1, True)
        round_w1(0, 0, V)
        round_w1(0, 1, S)
        quant_w1(0)
        first(1, 0)
        first(1, 1)
        round_w1(1, 0, S)
        round_w1(1, 1, S)
        quant_w1(1)
        second(0)
        second(1)
        for b in range(2):
            nc.sync.dma_start(out=out[b * P : (b + 1) * P, :], in_=placed[b][:])
